import numpy as np
import ml_dtypes


def mxq(x, axis, fmt="e4m3"):
    dtype, down = {"e4m3": (ml_dtypes.float8_e4m3fn, 7), "e5m2": (ml_dtypes.float8_e5m2, 14)}[fmt]
    v = np.moveaxis(np.asarray(x, np.float32).astype(ml_dtypes.bfloat16).astype(np.float64), axis, -1)
    blocks = v.reshape(v.shape[:-1] + (-1, 32))
    amax = np.abs(blocks).max(-1, keepdims=True)
    byte = np.maximum(np.where(amax > 0, np.frexp(amax)[1] - 1 + 127, 0) - down, 1)
    scale = np.exp2(byte - 127.0)
    codes = (blocks / scale).astype(np.float32).astype(dtype).astype(np.float64)
    return np.moveaxis((codes * scale).reshape(v.shape), -1, axis)


WIDE = False


def mx_kscale(k):
    if not WIDE:
        return np.ones(k)
    levels = np.array([10, -10, 5, -5, 0])
    if k % 512:
        return np.exp2(np.random.permutation(np.resize(levels, k // 32))).repeat(32)
    a = np.empty((k // 512, 16))
    for p in range(k // 512):
        a[p, :8] = np.random.permutation(np.resize(levels, 8))
        for g in range(8):
            far = levels[np.abs(levels - a[p, g]) >= 10]
            a[p, g + 8] = far[np.random.randint(len(far))]
    return np.exp2(a.ravel()).repeat(32)


def f64(x):
    return np.asarray(x).astype(np.float64)


def striped(idx):
    return np.tile(idx.reshape(-1, 16).T, (8, 1)).astype(np.uint16)


def unstriped(offs):
    return offs[:16].T.reshape(-1).astype(np.int64)


K, T, D, S, V, H, N = 1024, 1024, 2, 512, 256, 1024, 256
P = 2 ** 7


def setup_inputs():
    n = np.random.standard_normal
    s = mx_kscale(K)[:, None]
    u = mx_kscale(H)
    q = np.random.permutation(S)
    return {
        "xT": (n((K, T)) * s).astype(np.float32),
        "w1": (n((K, H)) / np.sqrt(K) / s * u).astype(np.float32),
        "w2": (n((H, N)) / np.sqrt(H) / u[:, None]).astype(np.float32),
        "gate": np.tile(np.random.uniform(0.2, 1.0, (D, 1, V)) / np.sqrt(D), (1, P, 1)).astype(np.float32),
        "offs": striped(np.random.permutation(T)[:S]),
        "pos1": striped(q[:V]),
        "pos2": striped(q[V:]),
    }


def reference(xT, w1, w2, gate, offs, pos1, pos2):
    h = mxq(f64(w1), 0, "e4m3").T @ mxq(f64(xT)[:, unstriped(offs)], 0, "e4m3")
    z = sum(f64(gate)[d, :1] * h[:, unstriped(p)] for d, p in enumerate((pos1, pos2)))
    return mxq(f64(w2), 0, "e4m3").T @ mxq(z, 0, "e4m3")

@@ -1,0 +1,234 @@
+from contextlib import ExitStack
+
+import concourse.mybir as mybir
+
+K, T, S, V, H, N = 1024, 1024, 512, 256, 1024, 256
+FLOPS = 2 * K * H * S + 2 * H * N * V
+
+F32 = mybir.dt.float32
+BF16 = mybir.dt.bfloat16
+U32 = mybir.dt.uint32
+U16 = mybir.dt.uint16
+U8 = mybir.dt.uint8
+FP8X4 = mybir.dt.float8_e4m3fn_x4
+ADD = mybir.AluOpType.add
+MULT = mybir.AluOpType.mult
+
+P = 128
+PACK = 4
+KP = P * PACK
+QUAD = 4
+
+X_SCALAR = ((64, 96), (512, 224))
+W_SCALAR = ((448, 320), (256, 512))
+
+
+def tile_picked_sage_none_e_kernel(tc, xT, w1, w2, gate, offs, pos1, pos2, out):
+    nc = tc.nc
+    with ExitStack() as ctx:
+        keep = ctx.enter_context(tc.tile_pool(name="keep", bufs=1))
+        h_psum = ctx.enter_context(tc.psum_pool(name="h_psum", bufs=1))
+        o_psum = ctx.enter_context(tc.psum_pool(name="o_psum", bufs=1))
+
+        offs_t = keep.tile([P, S // 16], U16, name="offs_t")
+        pos_t = [keep.tile([P, V // 16], U16, name=f"pos_t{d}") for d in range(2)]
+        gate_t = keep.tile([P, 2, V], F32, name="gate_t")
+
+        x_raw = [[keep.tile([P, PACK, 512], F32, name=f"x_raw{s}{c}") for c in range(2)] for s in range(2)]
+        x_bf = [[keep.tile([P, 512, PACK], BF16, name=f"x_bf{s}{c}", align_bytes=64) for c in range(2)] for s in range(2)]
+        x_codes = [keep.tile([P, T], U32, name=f"x_codes{s}", align_bytes=64) for s in range(2)]
+        x_scales = [keep.tile([P, T], U8, name=f"x_scales{s}", align_bytes=64) for s in range(2)]
+        g_codes = [keep.tile([P, S], U32, name=f"g_codes{s}", align_bytes=64) for s in range(2)]
+        g_scales = [keep.tile([P, S], U8, name=f"g_scales{s}", align_bytes=64) for s in range(2)]
+
+        w_raw = [[keep.tile([P, PACK, 512], F32, name=f"w_raw{g}{s}") for s in range(2)] for g in range(2)]
+        w_bf = [[keep.tile([P, 512 * PACK], BF16, name=f"w_bf{g}{s}", align_bytes=64) for s in range(2)] for g in range(2)]
+        w_codes = [[keep.tile([P, 512], U32, name=f"w_codes{g}{s}", align_bytes=64) for s in range(2)] for g in range(2)]
+        w_scales = [[keep.tile([P, 512], U8, name=f"w_scales{g}{s}", align_bytes=64) for s in range(2)] for g in range(2)]
+
+        v_raw = [keep.tile([P, PACK, N], F32, name=f"v_raw{g}") for g in range(2)]
+        v_bf = [keep.tile([P, N, PACK], BF16, name=f"v_bf{g}", align_bytes=64) for g in range(2)]
+        v_codes = [keep.tile([P, N], U32, name=f"v_codes{g}", align_bytes=64) for g in range(2)]
+        v_scales = [keep.tile([P, N], U8, name=f"v_scales{g}", align_bytes=64) for g in range(2)]
+
+        h = [[keep.tile([P, S], F32, name=f"h{g}{t}", align_bytes=64) for t in range(PACK)] for g in range(2)]
+        prod = [[keep.tile([P, PACK, V], F32, name=f"prod{g}{d}", align_bytes=64) for d in range(2)] for g in range(2)]
+        z_bf = [keep.tile([P, V, PACK], BF16, name=f"z_bf{g}", align_bytes=64) for g in range(2)]
+        z_codes = [keep.tile([P, V], U32, name=f"z_codes{g}", align_bytes=64) for g in range(2)]
+        z_scales = [keep.tile([P, V], U8, name=f"z_scales{g}", align_bytes=64) for g in range(2)]
+        o_sb = [keep.tile([P, V], F32, name=f"o_sb{m}") for m in range(2)]
+
+        banks = [h_psum.tile([P, S], F32, name=f"bank{b}") for b in range(6)]
+        o_bank = [o_psum.tile([P, V], F32, name=f"o_bank{m}") for m in range(2)]
+
+        for s in range(2):
+            nc.gpsimd.memset(x_scales[s][:], 0)
+
+        nc.sync.dma_start(offs_t[:], offs)
+        for s in range(2):
+            for c in range(2):
+                nc.sync.dma_start(
+                    out=x_raw[s][c][:],
+                    in_=xT[s * KP : (s + 1) * KP, c * 512 : (c + 1) * 512].rearrange("(p j) t -> p j t", j=PACK),
+                )
+        nc.sync.dma_start(pos_t[0][:], pos1)
+        nc.sync.dma_start(pos_t[1][:], pos2)
+        for g in range(2):
+            for s in range(2):
+                nc.sync.dma_start(
+                    out=w_raw[g][s][:],
+                    in_=w1[s * KP : (s + 1) * KP, g * 512 : (g + 1) * 512].rearrange("(p j) i -> p j i", j=PACK),
+                )
+            if g == 0:
+                nc.sync.dma_start(out=gate_t[:], in_=gate.rearrange("d p v -> p d v"))
+        for g in range(2):
+            nc.sync.dma_start(
+                out=v_raw[g][:], in_=w2[g * KP : (g + 1) * KP, :].rearrange("(p j) m -> p j m", j=PACK)
+            )
+
+        def interleave(dst, src, split):
+            width = src.shape[2]
+            for copy, lo, hi in ((nc.scalar.copy, 0, split), (nc.vector.tensor_copy, split, width)):
+                if hi > lo:
+                    copy(
+                        out=dst[:, lo:hi, :].rearrange("p (c i) t -> p c t i", i=QUAD),
+                        in_=src[:, :, lo:hi].rearrange("p t (c i) -> p c t i", i=QUAD),
+                    )
+
+        def interleave_permuted(dst, src, split):
+            d4 = dst.rearrange("p (t m j) -> p m j t", t=PACK, j=PACK)
+            s4 = src.rearrange("p j (m t) -> p m j t", t=PACK)
+            cut = split // PACK
+            for copy, lo, hi in ((nc.scalar.copy, 0, cut), (nc.vector.tensor_copy, cut, P)):
+                if hi > lo:
+                    copy(out=d4[:, lo:hi], in_=s4[:, lo:hi])
+
+        def quantize(codes, scales, src):
+            nc.vector.quantize_mx(out=codes.bitcast(FP8X4), scales=scales, in_=src)
+
+        def cast_x(s, c):
+            interleave(x_bf[s][c][:], x_raw[s][c][:], X_SCALAR[s][c])
+
+        def quant_x(s, c):
+            cols = slice(c * 512, (c + 1) * 512)
+            quantize(x_codes[s][:, cols], x_scales[s][:, cols], x_bf[s][c][:].rearrange("p n j -> p (n j)"))
+
+        def gather_x(s):
+            nc.vector.tensor_copy(g_codes[s][:], x_codes[s][:].indirect(offs_t[:]))
+            nc.vector.tensor_copy(g_scales[s][:], x_scales[s][:].indirect(offs_t[:]))
+
+        def cast_w(g, s):
+            interleave_permuted(w_bf[g][s][:], w_raw[g][s][:], W_SCALAR[g][s])
+
+        def quant_w(g, s, parts):
+            for lo in range(0, 512, 512 // parts):
+                cols = slice(lo, lo + 512 // parts)
+                raw = slice(lo * PACK, (lo + 512 // parts) * PACK)
+                quantize(w_codes[g][s][:, cols], w_scales[g][s][:, cols], w_bf[g][s][:, raw])
+
+        def bank_of(g, t):
+            return banks[(4 * g + t) % 6]
+
+        def layer1(g, s, t):
+            cols = slice(t * P, (t + 1) * P)
+            nc.tensor.matmul_mx(
+                out=bank_of(g, t)[:],
+                lhsT=w_codes[g][s][:, cols].bitcast(FP8X4),
+                lhsT_scale=w_scales[g][s][:, cols],
+                rhs=g_codes[s][:].bitcast(FP8X4),
+                rhs_scale=g_scales[s][:],
+                start=(s == 0),
+                stop=(s == 1),
+            )
+
+        def empty(g, t):
+            nc.scalar.copy(out=h[g][t][:], in_=bank_of(g, t)[:])
+
+        def neighbours(g, t):
+            for d in range(2):
+                nc.vector.tensor_tensor(
+                    prod[g][d][:, t, :], h[g][t][:].indirect(pos_t[d][:]), gate_t[:, d, :], MULT
+                )
+
+        def add(g):
+            view = "p t (c i) -> p c t i"
+            nc.vector.tensor_tensor(
+                out=z_bf[g][:].rearrange("p (c i) t -> p c t i", i=QUAD),
+                in0=prod[g][0][:].rearrange(view, i=QUAD),
+                in1=prod[g][1][:].rearrange(view, i=QUAD),
+                op=ADD,
+            )
+
+        def quant_z(g):
+            quantize(z_codes[g][:], z_scales[g][:], z_bf[g][:].rearrange("p n j -> p (n j)"))
+
+        def cast_v(g):
+            interleave(v_bf[g][:], v_raw[g][:], N)
+
+        def quant_v(g):
+            quantize(v_codes[g][:], v_scales[g][:], v_bf[g][:].rearrange("p n j -> p (n j)"))
+
+        def layer2(g, m):
+            cols = slice(m * P, (m + 1) * P)
+            nc.tensor.matmul_mx(
+                out=o_bank[m][:],
+                lhsT=v_codes[g][:, cols].bitcast(FP8X4),
+                lhsT_scale=v_scales[g][:, cols],
+                rhs=z_codes[g][:].bitcast(FP8X4),
+                rhs_scale=z_scales[g][:],
+                start=(g == 0),
+                stop=(g == 1),
+            )
+
+        cast_x(0, 0)
+        quant_x(0, 0)
+        cast_x(0, 1)
+        quant_x(0, 1)
+        cast_x(1, 0)
+        gather_x(0)
+        quant_x(1, 0)
+        cast_x(1, 1)
+        quant_x(1, 1)
+        cast_w(0, 0)
+        gather_x(1)
+        quant_w(0, 0, 1)
+        for t in range(PACK):
+            layer1(0, 0, t)
+        cast_w(0, 1)
+        quant_w(0, 1, 4)
+        for t in range(PACK):
+            layer1(0, 1, t)
+            empty(0, t)
+        cast_w(1, 0)
+        neighbours(0, 0)
+        neighbours(0, 1)
+        quant_w(1, 0, 1)
+        for t in range(PACK):
+            layer1(1, 0, t)
+        cast_w(1, 1)
+        neighbours(0, 2)
+        neighbours(0, 3)
+        quant_w(1, 1, 1)
+        for t in range(PACK):
+            layer1(1, 1, t)
+            empty(1, t)
+        cast_v(0)
+        cast_v(1)
+        add(0)
+        quant_v(0)
+        quant_z(0)
+        for m in range(2):
+            layer2(0, m)
+        neighbours(1, 0)
+        neighbours(1, 1)
+        quant_v(1)
+        neighbours(1, 2)
+        neighbours(1, 3)
+        add(1)
+        quant_z(1)
+        for m in range(2):
+            layer2(1, m)
+        nc.scalar.copy(out=o_sb[0][:], in_=o_bank[0][:])
+        nc.vector.tensor_copy(out=o_sb[1][:], in_=o_bank[1][:])
+        nc.sync.dma_start(out=out[0:P, :], in_=o_sb[0][:])
+        nc.scalar.dma_start(out=out[P : 2 * P, :], in_=o_sb[1][:])

@@ -19,8 +19,8 @@ PACK = 4
 KP = P * PACK
 QUAD = 4
 
-X_SCALAR = ((64, 96), (512, 224))
-W_SCALAR = ((448, 320), (256, 512))
+X_SCALAR = ((0, 192), (512, 160))
+W_SCALAR = ((512, 288), (0, 512))
 
 
 def tile_picked_sage_none_e_kernel(tc, xT, w1, w2, gate, offs, pos1, pos2, out):
@@ -37,12 +37,18 @@ def tile_picked_sage_none_e_kernel(tc, xT, w1, w2, gate, offs, pos1, pos2, out):
         x_raw = [[keep.tile([P, PACK, 512], F32, name=f"x_raw{s}{c}") for c in range(2)] for s in range(2)]
         x_bf = [[keep.tile([P, 512, PACK], BF16, name=f"x_bf{s}{c}", align_bytes=64) for c in range(2)] for s in range(2)]
         x_codes = [keep.tile([P, T], U32, name=f"x_codes{s}", align_bytes=64) for s in range(2)]
-        x_scales = [keep.tile([P, T], U8, name=f"x_scales{s}", align_bytes=64) for s in range(2)]
+        x_scales = keep.tile([P, T], U8, name="x_scales", align_bytes=64)
         g_codes = [keep.tile([P, S], U32, name=f"g_codes{s}", align_bytes=64) for s in range(2)]
-        g_scales = [keep.tile([P, S], U8, name=f"g_scales{s}", align_bytes=64) for s in range(2)]
+        g_scales = keep.tile([P, S], U8, name="g_scales", align_bytes=64)
 
-        w_raw = [[keep.tile([P, PACK, 512], F32, name=f"w_raw{g}{s}") for s in range(2)] for g in range(2)]
-        w_bf = [[keep.tile([P, 512 * PACK], BF16, name=f"w_bf{g}{s}", align_bytes=64) for s in range(2)] for g in range(2)]
+        w_raw = [
+            [keep.tile([P, PACK, 512], F32, name=f"w_raw{g}{s}", tag=f"w_raw{g}{s}", align_bytes=64) for s in range(2)]
+            for g in range(2)
+        ]
+        w_bf = [
+            [keep.tile([P, 512 * PACK], BF16, name=f"w_bf{g}{s}", tag=f"w_bf{g}{s}", align_bytes=64) for s in range(2)]
+            for g in range(2)
+        ]
         w_codes = [[keep.tile([P, 512], U32, name=f"w_codes{g}{s}", align_bytes=64) for s in range(2)] for g in range(2)]
         w_scales = [[keep.tile([P, 512], U8, name=f"w_scales{g}{s}", align_bytes=64) for s in range(2)] for g in range(2)]
 
@@ -51,8 +57,8 @@ def tile_picked_sage_none_e_kernel(tc, xT, w1, w2, gate, offs, pos1, pos2, out):
         v_codes = [keep.tile([P, N], U32, name=f"v_codes{g}", align_bytes=64) for g in range(2)]
         v_scales = [keep.tile([P, N], U8, name=f"v_scales{g}", align_bytes=64) for g in range(2)]
 
-        h = [[keep.tile([P, S], F32, name=f"h{g}{t}", align_bytes=64) for t in range(PACK)] for g in range(2)]
-        prod = [[keep.tile([P, PACK, V], F32, name=f"prod{g}{d}", align_bytes=64) for d in range(2)] for g in range(2)]
+        h = {}
+        prod = {}
         z_bf = [keep.tile([P, V, PACK], BF16, name=f"z_bf{g}", align_bytes=64) for g in range(2)]
         z_codes = [keep.tile([P, V], U32, name=f"z_codes{g}", align_bytes=64) for g in range(2)]
         z_scales = [keep.tile([P, V], U8, name=f"z_scales{g}", align_bytes=64) for g in range(2)]
@@ -61,8 +67,7 @@ def tile_picked_sage_none_e_kernel(tc, xT, w1, w2, gate, offs, pos1, pos2, out):
         banks = [h_psum.tile([P, S], F32, name=f"bank{b}") for b in range(6)]
         o_bank = [o_psum.tile([P, V], F32, name=f"o_bank{m}") for m in range(2)]
 
-        for s in range(2):
-            nc.gpsimd.memset(x_scales[s][:], 0)
+        nc.gpsimd.memset(x_scales[:], 0)
 
         nc.sync.dma_start(offs_t[:], offs)
         for s in range(2):
@@ -79,8 +84,8 @@ def tile_picked_sage_none_e_kernel(tc, xT, w1, w2, gate, offs, pos1, pos2, out):
                     out=w_raw[g][s][:],
                     in_=w1[s * KP : (s + 1) * KP, g * 512 : (g + 1) * 512].rearrange("(p j) i -> p j i", j=PACK),
                 )
-            if g == 0:
-                nc.sync.dma_start(out=gate_t[:], in_=gate.rearrange("d p v -> p d v"))
+                if (g, s) == (1, 1):
+                    nc.sync.dma_start(out=gate_t[:], in_=gate.rearrange("d p v -> p d v"))
         for g in range(2):
             nc.sync.dma_start(
                 out=v_raw[g][:], in_=w2[g * KP : (g + 1) * KP, :].rearrange("(p j) m -> p j m", j=PACK)
@@ -111,11 +116,13 @@ def tile_picked_sage_none_e_kernel(tc, xT, w1, w2, gate, offs, pos1, pos2, out):
 
         def quant_x(s, c):
             cols = slice(c * 512, (c + 1) * 512)
-            quantize(x_codes[s][:, cols], x_scales[s][:, cols], x_bf[s][c][:].rearrange("p n j -> p (n j)"))
+            quantize(x_codes[s][:, cols], x_scales[PACK * s : P, cols], x_bf[s][c][:].rearrange("p n j -> p (n j)"))
 
-        def gather_x(s):
+        def gather_codes(s):
             nc.vector.tensor_copy(g_codes[s][:], x_codes[s][:].indirect(offs_t[:]))
-            nc.vector.tensor_copy(g_scales[s][:], x_scales[s][:].indirect(offs_t[:]))
+
+        def gather_scales():
+            nc.vector.tensor_copy(g_scales[:], x_scales[:].indirect(offs_t[:]))
 
         def cast_w(g, s):
             interleave_permuted(w_bf[g][s][:], w_raw[g][s][:], W_SCALAR[g][s])
@@ -136,18 +143,24 @@ def tile_picked_sage_none_e_kernel(tc, xT, w1, w2, gate, offs, pos1, pos2, out):
                 lhsT=w_codes[g][s][:, cols].bitcast(FP8X4),
                 lhsT_scale=w_scales[g][s][:, cols],
                 rhs=g_codes[s][:].bitcast(FP8X4),
-                rhs_scale=g_scales[s][:],
+                rhs_scale=g_scales[PACK * s : P, :],
                 start=(s == 0),
                 stop=(s == 1),
             )
 
-        def empty(g, t):
-            nc.scalar.copy(out=h[g][t][:], in_=bank_of(g, t)[:])
+        def empty(g, t, tag=None):
+            h[g, t] = keep.tile([P, S], F32, name=f"h{g}{t}", tag=tag or f"h{g}{t}", align_bytes=64)
+            nc.scalar.copy(out=h[g, t][:], in_=bank_of(g, t)[:])
 
-        def neighbours(g, t):
-            for d in range(2):
+        def products(g, tags):
+            prod[g] = [
+                keep.tile([P, PACK, V], F32, name=f"prod{g}{d}", tag=tag, align_bytes=64) for d, tag in enumerate(tags)
+            ]
+
+        def neighbours(g, t, turns=(0, 1)):
+            for d in turns:
                 nc.vector.tensor_tensor(
-                    prod[g][d][:, t, :], h[g][t][:].indirect(pos_t[d][:]), gate_t[:, d, :], MULT
+                    prod[g][d][:, t, :], h[g, t][:].indirect(pos_t[d][:]), gate_t[:, d, :], MULT
                 )
 
         def add(g):
@@ -184,47 +197,60 @@ def tile_picked_sage_none_e_kernel(tc, xT, w1, w2, gate, offs, pos1, pos2, out):
         quant_x(0, 0)
         cast_x(0, 1)
         quant_x(0, 1)
+        gather_codes(0)
         cast_x(1, 0)
-        gather_x(0)
-        quant_x(1, 0)
         cast_x(1, 1)
+        quant_x(1, 0)
         quant_x(1, 1)
         cast_w(0, 0)
-        gather_x(1)
+        gather_scales()
+        gather_codes(1)
         quant_w(0, 0, 1)
-        for t in range(PACK):
-            layer1(0, 0, t)
         cast_w(0, 1)
         quant_w(0, 1, 4)
-        for t in range(PACK):
+        cast_w(1, 0)
+        quant_w(1, 0, 1)
+        for t in range(2):
+            layer1(0, 0, t)
             layer1(0, 1, t)
             empty(0, t)
-        cast_w(1, 0)
+        products(0, ("w_bf10", "prod01"))
         neighbours(0, 0)
-        neighbours(0, 1)
-        quant_w(1, 0, 1)
-        for t in range(PACK):
-            layer1(1, 0, t)
+        neighbours(0, 1, (0,))
         cast_w(1, 1)
-        neighbours(0, 2)
-        neighbours(0, 3)
+        layer1(0, 0, 2)
+        layer1(0, 1, 2)
+        empty(0, 2, "w_raw11")
+        layer1(1, 0, 0)
+        layer1(0, 0, 3)
+        layer1(0, 1, 3)
+        layer1(1, 0, 1)
+        neighbours(0, 1, (1,))
         quant_w(1, 1, 1)
-        for t in range(PACK):
+        neighbours(0, 2)
+        empty(0, 3)
+        for t in range(2):
             layer1(1, 1, t)
             empty(1, t)
         cast_v(0)
+        neighbours(0, 3)
+        for t in range(2, PACK):
+            layer1(1, 0, t)
+            layer1(1, 1, t)
+            empty(1, t)
         cast_v(1)
-        add(0)
+        products(1, ("prod10", "prod11"))
+        neighbours(1, 0)
         quant_v(0)
+        neighbours(1, 1)
+        add(0)
+        neighbours(1, 2)
+        neighbours(1, 3)
         quant_z(0)
         for m in range(2):
             layer2(0, m)
-        neighbours(1, 0)
-        neighbours(1, 1)
-        quant_v(1)
-        neighbours(1, 2)
-        neighbours(1, 3)
         add(1)
+        quant_v(1)
         quant_z(1)
         for m in range(2):
             layer2(1, m)

@@ -19,8 +19,8 @@ PACK = 4
 KP = P * PACK
 QUAD = 4
 
-X_SCALAR = ((0, 192), (512, 160))
-W_SCALAR = ((512, 288), (0, 512))
+X_SCALAR = (352, 288)
+W_SCALAR = ((480, 352), (0, 512))
 
 
 def tile_picked_sage_none_e_kernel(tc, xT, w1, w2, gate, offs, pos1, pos2, out):
@@ -34,8 +34,8 @@ def tile_picked_sage_none_e_kernel(tc, xT, w1, w2, gate, offs, pos1, pos2, out):
         pos_t = [keep.tile([P, V // 16], U16, name=f"pos_t{d}") for d in range(2)]
         gate_t = keep.tile([P, 2, V], F32, name="gate_t")
 
-        x_raw = [[keep.tile([P, PACK, 512], F32, name=f"x_raw{s}{c}") for c in range(2)] for s in range(2)]
-        x_bf = [[keep.tile([P, 512, PACK], BF16, name=f"x_bf{s}{c}", align_bytes=64) for c in range(2)] for s in range(2)]
+        x_raw = [keep.tile([P, PACK, T], F32, name=f"x_raw{s}") for s in range(2)]
+        x_bf = [keep.tile([P, T, PACK], BF16, name=f"x_bf{s}", align_bytes=64) for s in range(2)]
         x_codes = [keep.tile([P, T], U32, name=f"x_codes{s}", align_bytes=64) for s in range(2)]
         x_scales = keep.tile([P, T], U8, name="x_scales", align_bytes=64)
         g_codes = [keep.tile([P, S], U32, name=f"g_codes{s}", align_bytes=64) for s in range(2)]
@@ -71,11 +71,7 @@ def tile_picked_sage_none_e_kernel(tc, xT, w1, w2, gate, offs, pos1, pos2, out):
 
         nc.sync.dma_start(offs_t[:], offs)
         for s in range(2):
-            for c in range(2):
-                nc.sync.dma_start(
-                    out=x_raw[s][c][:],
-                    in_=xT[s * KP : (s + 1) * KP, c * 512 : (c + 1) * 512].rearrange("(p j) t -> p j t", j=PACK),
-                )
+            nc.sync.dma_start(out=x_raw[s][:], in_=xT[s * KP : (s + 1) * KP, :].rearrange("(p j) t -> p j t", j=PACK))
         nc.sync.dma_start(pos_t[0][:], pos1)
         nc.sync.dma_start(pos_t[1][:], pos2)
         for g in range(2):
@@ -111,12 +107,12 @@ def tile_picked_sage_none_e_kernel(tc, xT, w1, w2, gate, offs, pos1, pos2, out):
         def quantize(codes, scales, src):
             nc.vector.quantize_mx(out=codes.bitcast(FP8X4), scales=scales, in_=src)
 
-        def cast_x(s, c):
-            interleave(x_bf[s][c][:], x_raw[s][c][:], X_SCALAR[s][c])
+        def cast_x(s):
+            interleave(x_bf[s][:], x_raw[s][:], X_SCALAR[s])
 
         def quant_x(s, c):
             cols = slice(c * 512, (c + 1) * 512)
-            quantize(x_codes[s][:, cols], x_scales[PACK * s : P, cols], x_bf[s][c][:].rearrange("p n j -> p (n j)"))
+            quantize(x_codes[s][:, cols], x_scales[PACK * s : P, cols], x_bf[s][:, cols, :].rearrange("p n j -> p (n j)"))
 
         def gather_codes(s):
             nc.vector.tensor_copy(g_codes[s][:], x_codes[s][:].indirect(offs_t[:]))
@@ -193,15 +189,13 @@ def tile_picked_sage_none_e_kernel(tc, xT, w1, w2, gate, offs, pos1, pos2, out):
                 stop=(g == 1),
             )
 
-        cast_x(0, 0)
-        quant_x(0, 0)
-        cast_x(0, 1)
+        cast_x(0)
         quant_x(0, 1)
+        quant_x(0, 0)
         gather_codes(0)
-        cast_x(1, 0)
-        cast_x(1, 1)
-        quant_x(1, 0)
+        cast_x(1)
         quant_x(1, 1)
+        quant_x(1, 0)
         cast_w(0, 0)
         gather_scales()
         gather_codes(1)

@@ -19,8 +19,8 @@ PACK = 4
 KP = P * PACK
 QUAD = 4
 
-X_SCALAR = (352, 288)
-W_SCALAR = ((480, 352), (0, 512))
+X_SCALAR = (416, 480, 160)
+W_SCALAR = ((480, 320), (0, 512))
 
 
 def tile_picked_sage_none_e_kernel(tc, xT, w1, w2, gate, offs, pos1, pos2, out):
@@ -34,7 +34,7 @@ def tile_picked_sage_none_e_kernel(tc, xT, w1, w2, gate, offs, pos1, pos2, out):
         pos_t = [keep.tile([P, V // 16], U16, name=f"pos_t{d}") for d in range(2)]
         gate_t = keep.tile([P, 2, V], F32, name="gate_t")
 
-        x_raw = [keep.tile([P, PACK, T], F32, name=f"x_raw{s}") for s in range(2)]
+        x_raw = [keep.tile([P, PACK, w], F32, name=f"x_raw{i}") for i, w in enumerate((T, 512, 512))]
         x_bf = [keep.tile([P, T, PACK], BF16, name=f"x_bf{s}", align_bytes=64) for s in range(2)]
         x_codes = [keep.tile([P, T], U32, name=f"x_codes{s}", align_bytes=64) for s in range(2)]
         x_scales = keep.tile([P, T], U8, name="x_scales", align_bytes=64)
@@ -69,19 +69,26 @@ def tile_picked_sage_none_e_kernel(tc, xT, w1, w2, gate, offs, pos1, pos2, out):
 
         nc.gpsimd.memset(x_scales[:], 0)
 
+        def load_w(g, s):
+            nc.sync.dma_start(
+                out=w_raw[g][s][:],
+                in_=w1[s * KP : (s + 1) * KP, g * 512 : (g + 1) * 512].rearrange("(p j) i -> p j i", j=PACK),
+            )
+
+        nc.sync.dma_start(out=x_raw[0][:], in_=xT[0:KP, :].rearrange("(p j) t -> p j t", j=PACK))
         nc.sync.dma_start(offs_t[:], offs)
-        for s in range(2):
-            nc.sync.dma_start(out=x_raw[s][:], in_=xT[s * KP : (s + 1) * KP, :].rearrange("(p j) t -> p j t", j=PACK))
+        for c in range(2):
+            cols = slice(c * 512, (c + 1) * 512)
+            nc.sync.dma_start(
+                out=x_raw[1 + c][:], in_=xT[KP : 2 * KP, cols].rearrange("(p j) t -> p j t", j=PACK)
+            )
+        load_w(0, 0)
+        load_w(0, 1)
+        load_w(1, 0)
         nc.sync.dma_start(pos_t[0][:], pos1)
         nc.sync.dma_start(pos_t[1][:], pos2)
-        for g in range(2):
-            for s in range(2):
-                nc.sync.dma_start(
-                    out=w_raw[g][s][:],
-                    in_=w1[s * KP : (s + 1) * KP, g * 512 : (g + 1) * 512].rearrange("(p j) i -> p j i", j=PACK),
-                )
-                if (g, s) == (1, 1):
-                    nc.sync.dma_start(out=gate_t[:], in_=gate.rearrange("d p v -> p d v"))
+        load_w(1, 1)
+        nc.sync.dma_start(out=gate_t[:], in_=gate.rearrange("d p v -> p d v"))
         for g in range(2):
             nc.sync.dma_start(
                 out=v_raw[g][:], in_=w2[g * KP : (g + 1) * KP, :].rearrange("(p j) m -> p j m", j=PACK)
@@ -107,8 +114,9 @@ def tile_picked_sage_none_e_kernel(tc, xT, w1, w2, gate, offs, pos1, pos2, out):
         def quantize(codes, scales, src):
             nc.vector.quantize_mx(out=codes.bitcast(FP8X4), scales=scales, in_=src)
 
-        def cast_x(s):
-            interleave(x_bf[s][:], x_raw[s][:], X_SCALAR[s])
+        def cast_x(i):
+            dst = x_bf[0][:] if i == 0 else x_bf[1][:, (i - 1) * 512 : i * 512, :]
+            interleave(dst, x_raw[i][:], X_SCALAR[i])
 
         def quant_x(s, c):
             cols = slice(c * 512, (c + 1) * 512)
@@ -194,8 +202,9 @@ def tile_picked_sage_none_e_kernel(tc, xT, w1, w2, gate, offs, pos1, pos2, out):
         quant_x(0, 0)
         gather_codes(0)
         cast_x(1)
-        quant_x(1, 1)
+        cast_x(2)
         quant_x(1, 0)
+        quant_x(1, 1)
         cast_w(0, 0)
         gather_scales()
         gather_codes(1)

@@ -20,7 +20,7 @@ KP = P * PACK
 QUAD = 4
 
 X_SCALAR = (416, 480, 160)
-W_SCALAR = ((480, 320), (0, 512))
+W_SCALAR = ((512, 256), (0, 512))
 
 
 def tile_picked_sage_none_e_kernel(tc, xT, w1, w2, gate, offs, pos1, pos2, out):
@@ -87,8 +87,8 @@ def tile_picked_sage_none_e_kernel(tc, xT, w1, w2, gate, offs, pos1, pos2, out):
         load_w(1, 0)
         nc.sync.dma_start(pos_t[0][:], pos1)
         nc.sync.dma_start(pos_t[1][:], pos2)
-        load_w(1, 1)
         nc.sync.dma_start(out=gate_t[:], in_=gate.rearrange("d p v -> p d v"))
+        load_w(1, 1)
         for g in range(2):
             nc.sync.dma_start(
                 out=v_raw[g][:], in_=w2[g * KP : (g + 1) * KP, :].rearrange("(p j) m -> p j m", j=PACK)
@@ -161,8 +161,8 @@ def tile_picked_sage_none_e_kernel(tc, xT, w1, w2, gate, offs, pos1, pos2, out):
                 keep.tile([P, PACK, V], F32, name=f"prod{g}{d}", tag=tag, align_bytes=64) for d, tag in enumerate(tags)
             ]
 
-        def neighbours(g, t, turns=(0, 1)):
-            for d in turns:
+        def neighbours(g, t):
+            for d in range(2):
                 nc.vector.tensor_tensor(
                     prod[g][d][:, t, :], h[g, t][:].indirect(pos_t[d][:]), gate_t[:, d, :], MULT
                 )
@@ -219,36 +219,35 @@ def tile_picked_sage_none_e_kernel(tc, xT, w1, w2, gate, offs, pos1, pos2, out):
             empty(0, t)
         products(0, ("w_bf10", "prod01"))
         neighbours(0, 0)
-        neighbours(0, 1, (0,))
-        cast_w(1, 1)
+        neighbours(0, 1)
         layer1(0, 0, 2)
         layer1(0, 1, 2)
-        empty(0, 2, "w_raw11")
-        layer1(1, 0, 0)
+        empty(0, 2)
+        cast_w(1, 1)
         layer1(0, 0, 3)
         layer1(0, 1, 3)
-        layer1(1, 0, 1)
-        neighbours(0, 1, (1,))
-        quant_w(1, 1, 1)
+        for t in range(3):
+            layer1(1, 0, t)
         neighbours(0, 2)
-        empty(0, 3)
+        quant_w(1, 1, 1)
+        empty(0, 3, "w_raw11")
         for t in range(2):
             layer1(1, 1, t)
             empty(1, t)
-        cast_v(0)
         neighbours(0, 3)
-        for t in range(2, PACK):
-            layer1(1, 0, t)
-            layer1(1, 1, t)
-            empty(1, t)
+        cast_v(0)
+        layer1(1, 1, 2)
+        empty(1, 2)
+        layer1(1, 0, 3)
+        layer1(1, 1, 3)
+        empty(1, 3)
         cast_v(1)
+        add(0)
         products(1, ("prod10", "prod11"))
         neighbours(1, 0)
         quant_v(0)
-        neighbours(1, 1)
-        add(0)
-        neighbours(1, 2)
-        neighbours(1, 3)
+        for t in range(1, PACK):
+            neighbours(1, t)
         quant_z(0)
         for m in range(2):
             layer2(0, m)

from contextlib import ExitStack

import concourse.mybir as mybir

K, T, S, V, H, N = 1024, 1024, 512, 256, 1024, 256
FLOPS = 2 * K * H * S + 2 * H * N * V

F32 = mybir.dt.float32
BF16 = mybir.dt.bfloat16
U32 = mybir.dt.uint32
U16 = mybir.dt.uint16
U8 = mybir.dt.uint8
FP8X4 = mybir.dt.float8_e4m3fn_x4
ADD = mybir.AluOpType.add
MULT = mybir.AluOpType.mult

P = 128
PACK = 4
KP = P * PACK
QUAD = 4

X_SCALAR = (416, 480, 160)
W_SCALAR = ((512, 256), (0, 512))


def tile_picked_sage_none_e_kernel(tc, xT, w1, w2, gate, offs, pos1, pos2, out):
    nc = tc.nc
    with ExitStack() as ctx:
        keep = ctx.enter_context(tc.tile_pool(name="keep", bufs=1))
        h_psum = ctx.enter_context(tc.psum_pool(name="h_psum", bufs=1))
        o_psum = ctx.enter_context(tc.psum_pool(name="o_psum", bufs=1))

        offs_t = keep.tile([P, S // 16], U16, name="offs_t")
        pos_t = [keep.tile([P, V // 16], U16, name=f"pos_t{d}") for d in range(2)]
        gate_t = keep.tile([P, 2, V], F32, name="gate_t")

        x_raw = [keep.tile([P, PACK, w], F32, name=f"x_raw{i}") for i, w in enumerate((T, 512, 512))]
        x_bf = [keep.tile([P, T, PACK], BF16, name=f"x_bf{s}", align_bytes=64) for s in range(2)]
        x_codes = [keep.tile([P, T], U32, name=f"x_codes{s}", align_bytes=64) for s in range(2)]
        x_scales = keep.tile([P, T], U8, name="x_scales", align_bytes=64)
        g_codes = [keep.tile([P, S], U32, name=f"g_codes{s}", align_bytes=64) for s in range(2)]
        g_scales = keep.tile([P, S], U8, name="g_scales", align_bytes=64)

        w_raw = [
            [keep.tile([P, PACK, 512], F32, name=f"w_raw{g}{s}", tag=f"w_raw{g}{s}", align_bytes=64) for s in range(2)]
            for g in range(2)
        ]
        w_bf = [
            [keep.tile([P, 512 * PACK], BF16, name=f"w_bf{g}{s}", tag=f"w_bf{g}{s}", align_bytes=64) for s in range(2)]
            for g in range(2)
        ]
        w_codes = [[keep.tile([P, 512], U32, name=f"w_codes{g}{s}", align_bytes=64) for s in range(2)] for g in range(2)]
        w_scales = [[keep.tile([P, 512], U8, name=f"w_scales{g}{s}", align_bytes=64) for s in range(2)] for g in range(2)]

        v_raw = [keep.tile([P, PACK, N], F32, name=f"v_raw{g}") for g in range(2)]
        v_bf = [keep.tile([P, N, PACK], BF16, name=f"v_bf{g}", align_bytes=64) for g in range(2)]
        v_codes = [keep.tile([P, N], U32, name=f"v_codes{g}", align_bytes=64) for g in range(2)]
        v_scales = [keep.tile([P, N], U8, name=f"v_scales{g}", align_bytes=64) for g in range(2)]

        h = {}
        prod = {}
        z_bf = [keep.tile([P, V, PACK], BF16, name=f"z_bf{g}", align_bytes=64) for g in range(2)]
        z_codes = [keep.tile([P, V], U32, name=f"z_codes{g}", align_bytes=64) for g in range(2)]
        z_scales = [keep.tile([P, V], U8, name=f"z_scales{g}", align_bytes=64) for g in range(2)]
        o_sb = [keep.tile([P, V], F32, name=f"o_sb{m}") for m in range(2)]

        banks = [h_psum.tile([P, S], F32, name=f"bank{b}") for b in range(6)]
        o_bank = [o_psum.tile([P, V], F32, name=f"o_bank{m}") for m in range(2)]

        nc.gpsimd.memset(x_scales[:], 0)

        def load_w(g, s):
            nc.sync.dma_start(
                out=w_raw[g][s][:],
                in_=w1[s * KP : (s + 1) * KP, g * 512 : (g + 1) * 512].rearrange("(p j) i -> p j i", j=PACK),
            )

        nc.sync.dma_start(out=x_raw[0][:], in_=xT[0:KP, :].rearrange("(p j) t -> p j t", j=PACK))
        nc.sync.dma_start(offs_t[:], offs)
        for c in range(2):
            cols = slice(c * 512, (c + 1) * 512)
            nc.sync.dma_start(
                out=x_raw[1 + c][:], in_=xT[KP : 2 * KP, cols].rearrange("(p j) t -> p j t", j=PACK)
            )
        load_w(0, 0)
        load_w(0, 1)
        load_w(1, 0)
        nc.sync.dma_start(pos_t[0][:], pos1)
        nc.sync.dma_start(pos_t[1][:], pos2)
        nc.sync.dma_start(out=gate_t[:], in_=gate.rearrange("d p v -> p d v"))
        load_w(1, 1)
        for g in range(2):
            nc.sync.dma_start(
                out=v_raw[g][:], in_=w2[g * KP : (g + 1) * KP, :].rearrange("(p j) m -> p j m", j=PACK)
            )

        def interleave(dst, src, split):
            width = src.shape[2]
            for copy, lo, hi in ((nc.scalar.copy, 0, split), (nc.vector.tensor_copy, split, width)):
                if hi > lo:
                    copy(
                        out=dst[:, lo:hi, :].rearrange("p (c i) t -> p c t i", i=QUAD),
                        in_=src[:, :, lo:hi].rearrange("p t (c i) -> p c t i", i=QUAD),
                    )

        def interleave_permuted(dst, src, split):
            d4 = dst.rearrange("p (t m j) -> p m j t", t=PACK, j=PACK)
            s4 = src.rearrange("p j (m t) -> p m j t", t=PACK)
            cut = split // PACK
            for copy, lo, hi in ((nc.scalar.copy, 0, cut), (nc.vector.tensor_copy, cut, P)):
                if hi > lo:
                    copy(out=d4[:, lo:hi], in_=s4[:, lo:hi])

        def quantize(codes, scales, src):
            nc.vector.quantize_mx(out=codes.bitcast(FP8X4), scales=scales, in_=src)

        def cast_x(i):
            dst = x_bf[0][:] if i == 0 else x_bf[1][:, (i - 1) * 512 : i * 512, :]
            interleave(dst, x_raw[i][:], X_SCALAR[i])

        def quant_x(s, c):
            cols = slice(c * 512, (c + 1) * 512)
            quantize(x_codes[s][:, cols], x_scales[PACK * s : P, cols], x_bf[s][:, cols, :].rearrange("p n j -> p (n j)"))

        def gather_codes(s):
            nc.vector.tensor_copy(g_codes[s][:], x_codes[s][:].indirect(offs_t[:]))

        def gather_scales():
            nc.vector.tensor_copy(g_scales[:], x_scales[:].indirect(offs_t[:]))

        def cast_w(g, s):
            interleave_permuted(w_bf[g][s][:], w_raw[g][s][:], W_SCALAR[g][s])

        def quant_w(g, s, parts):
            for lo in range(0, 512, 512 // parts):
                cols = slice(lo, lo + 512 // parts)
                raw = slice(lo * PACK, (lo + 512 // parts) * PACK)
                quantize(w_codes[g][s][:, cols], w_scales[g][s][:, cols], w_bf[g][s][:, raw])

        def bank_of(g, t):
            return banks[(4 * g + t) % 6]

        def layer1(g, s, t):
            cols = slice(t * P, (t + 1) * P)
            nc.tensor.matmul_mx(
                out=bank_of(g, t)[:],
                lhsT=w_codes[g][s][:, cols].bitcast(FP8X4),
                lhsT_scale=w_scales[g][s][:, cols],
                rhs=g_codes[s][:].bitcast(FP8X4),
                rhs_scale=g_scales[PACK * s : P, :],
                start=(s == 0),
                stop=(s == 1),
            )

        def empty(g, t, tag=None):
            h[g, t] = keep.tile([P, S], F32, name=f"h{g}{t}", tag=tag or f"h{g}{t}", align_bytes=64)
            nc.scalar.copy(out=h[g, t][:], in_=bank_of(g, t)[:])

        def products(g, tags):
            prod[g] = [
                keep.tile([P, PACK, V], F32, name=f"prod{g}{d}", tag=tag, align_bytes=64) for d, tag in enumerate(tags)
            ]

        def neighbours(g, t):
            for d in range(2):
                nc.vector.tensor_tensor(
                    prod[g][d][:, t, :], h[g, t][:].indirect(pos_t[d][:]), gate_t[:, d, :], MULT
                )

        def add(g):
            view = "p t (c i) -> p c t i"
            nc.vector.tensor_tensor(
                out=z_bf[g][:].rearrange("p (c i) t -> p c t i", i=QUAD),
                in0=prod[g][0][:].rearrange(view, i=QUAD),
                in1=prod[g][1][:].rearrange(view, i=QUAD),
                op=ADD,
            )

        def quant_z(g):
            quantize(z_codes[g][:], z_scales[g][:], z_bf[g][:].rearrange("p n j -> p (n j)"))

        def cast_v(g):
            interleave(v_bf[g][:], v_raw[g][:], N)

        def quant_v(g):
            quantize(v_codes[g][:], v_scales[g][:], v_bf[g][:].rearrange("p n j -> p (n j)"))

        def layer2(g, m):
            cols = slice(m * P, (m + 1) * P)
            nc.tensor.matmul_mx(
                out=o_bank[m][:],
                lhsT=v_codes[g][:, cols].bitcast(FP8X4),
                lhsT_scale=v_scales[g][:, cols],
                rhs=z_codes[g][:].bitcast(FP8X4),
                rhs_scale=z_scales[g][:],
                start=(g == 0),
                stop=(g == 1),
            )

        cast_x(0)
        quant_x(0, 1)
        quant_x(0, 0)
        gather_codes(0)
        cast_x(1)
        cast_x(2)
        quant_x(1, 0)
        quant_x(1, 1)
        cast_w(0, 0)
        gather_scales()
        gather_codes(1)
        quant_w(0, 0, 1)
        cast_w(0, 1)
        quant_w(0, 1, 4)
        cast_w(1, 0)
        quant_w(1, 0, 1)
        for t in range(2):
            layer1(0, 0, t)
            layer1(0, 1, t)
            empty(0, t)
        products(0, ("w_bf10", "prod01"))
        neighbours(0, 0)
        neighbours(0, 1)
        layer1(0, 0, 2)
        layer1(0, 1, 2)
        empty(0, 2)
        cast_w(1, 1)
        layer1(0, 0, 3)
        layer1(0, 1, 3)
        for t in range(3):
            layer1(1, 0, t)
        neighbours(0, 2)
        quant_w(1, 1, 1)
        empty(0, 3, "w_raw11")
        for t in range(2):
            layer1(1, 1, t)
            empty(1, t)
        neighbours(0, 3)
        cast_v(0)
        layer1(1, 1, 2)
        empty(1, 2)
        layer1(1, 0, 3)
        layer1(1, 1, 3)
        empty(1, 3)
        cast_v(1)
        add(0)
        products(1, ("prod10", "prod11"))
        neighbours(1, 0)
        quant_v(0)
        for t in range(1, PACK):
            neighbours(1, t)
        quant_z(0)
        for m in range(2):
            layer2(0, m)
        add(1)
        quant_v(1)
        quant_z(1)
        for m in range(2):
            layer2(1, m)
        nc.scalar.copy(out=o_sb[0][:], in_=o_bank[0][:])
        nc.vector.tensor_copy(out=o_sb[1][:], in_=o_bank[1][:])
        nc.sync.dma_start(out=out[0:P, :], in_=o_sb[0][:])
        nc.scalar.dma_start(out=out[P : 2 * P, :], in_=o_sb[1][:])
